import numpy as np
import ml_dtypes


def mxq(x, axis, fmt="e4m3"):
    dtype, down = {"e4m3": (ml_dtypes.float8_e4m3fn, 7), "e5m2": (ml_dtypes.float8_e5m2, 14)}[fmt]
    v = np.moveaxis(np.asarray(x, np.float32).astype(ml_dtypes.bfloat16).astype(np.float64), axis, -1)
    blocks = v.reshape(v.shape[:-1] + (-1, 32))
    amax = np.abs(blocks).max(-1, keepdims=True)
    byte = np.maximum(np.where(amax > 0, np.frexp(amax)[1] - 1 + 127, 0) - down, 1)
    scale = np.exp2(byte - 127.0)
    codes = (blocks / scale).astype(np.float32).astype(dtype).astype(np.float64)
    return np.moveaxis((codes * scale).reshape(v.shape), -1, axis)


WIDE = False


def mx_kscale(k):
    if not WIDE:
        return np.ones(k)
    levels = np.array([10, -10, 5, -5, 0])
    if k % 512:
        return np.exp2(np.random.permutation(np.resize(levels, k // 32))).repeat(32)
    a = np.empty((k // 512, 16))
    for p in range(k // 512):
        a[p, :8] = np.random.permutation(np.resize(levels, 8))
        for g in range(8):
            far = levels[np.abs(levels - a[p, g]) >= 10]
            a[p, g + 8] = far[np.random.randint(len(far))]
    return np.exp2(a.ravel()).repeat(32)


def f64(x):
    return np.asarray(x).astype(np.float64)


def striped(idx):
    return np.tile(idx.reshape(-1, 16).T, (8, 1)).astype(np.uint16)


def unstriped(offs):
    return offs[:16].T.reshape(-1).astype(np.int64)


def striped8(idx):
    return np.concatenate([x.reshape(-1, 16).T for x in idx]).astype(np.uint16)


def runs(offs, k):
    lists = np.stack([offs[16 * r : 16 * r + 16].T.reshape(-1) for r in range(8)]).astype(np.int64)
    return lists[np.arange(k) % 512 // 64]


def pack_weight(w):
    k, n = w.shape
    w = f64(np.asarray(w, np.float32).astype(ml_dtypes.bfloat16)).reshape(k // 32, 32, n)
    amax = np.abs(w).max(1)
    byte = np.clip(np.where(amax > 0, np.frexp(amax)[1] - 1 + 127 - 7, 1), 1, 254)
    scaled = (w * np.exp2(127.0 - byte)[:, None, :]).reshape(k, n).astype(np.float32)
    words = np.ascontiguousarray(scaled.reshape(k // 512, 128, 4, n).transpose(0, 1, 3, 2)).astype(ml_dtypes.float8_e4m3fn).view(np.uint8)
    return words, np.ascontiguousarray(byte.astype(np.uint8).reshape(k // 512, 16, n))


def unpack_weight(words, scales):
    g, p, n, _ = words.shape
    vals = np.ascontiguousarray(words).view(ml_dtypes.float8_e4m3fn).astype(np.float64) * np.repeat(np.exp2(scales.astype(np.float64) - 127.0), 8, axis=1)[..., None]
    return vals.transpose(0, 1, 3, 2).reshape(g * 512, n)


E2M1 = np.array([0.0, 0.5, 1.0, 1.5, 2.0, 3.0, 4.0, 6.0, -0.0, -0.5, -1.0, -1.5, -2.0, -3.0, -4.0, -6.0])


def pack_fp4(w):
    k, n = w.shape
    w = f64(np.asarray(w, np.float32).astype(ml_dtypes.bfloat16)).reshape(k // 32, 32, n)
    amax = np.abs(w).max(1)
    mant, ex = np.frexp(amax / 6.0)
    byte = np.clip(np.where(amax > 0, np.where(mant > 0.5, ex, ex - 1) + 127, 1), 1, 254)
    scaled = (w * np.exp2(127.0 - byte)[:, None, :]).reshape(k, n).astype(np.float32)
    c = np.ascontiguousarray(scaled.reshape(k // 512, 128, 4, n).transpose(0, 1, 3, 2)).astype(ml_dtypes.float4_e2m1fn).view(np.uint8) & 0xF
    words = (c[..., 0::2] | (c[..., 1::2] << 4)).reshape(k // 512, 128, 2 * n)
    return np.ascontiguousarray(words), np.ascontiguousarray(byte.astype(np.uint8).reshape(k // 512, 16, n))


def unpack_fp4(words, scales):
    g, _, n = scales.shape
    words = np.ascontiguousarray(words).reshape(g, 128, n, 2)
    nib = np.empty((g, 128, n, 4), np.uint8)
    nib[..., 0::2] = words & 0xF
    nib[..., 1::2] = words >> 4
    vals = E2M1[nib] * np.repeat(np.exp2(scales.astype(np.float64) - 127.0), 8, axis=1)[..., None]
    return vals.transpose(0, 1, 3, 2).reshape(g * 512, n)


def planes(y):
    n, m = y.shape
    v = y.astype(np.float32).astype(ml_dtypes.bfloat16).astype(np.float64).reshape(n // 32, 32, m)
    top = np.abs(v).max(1)
    byte = np.clip(np.where(top > 0, np.frexp(top)[1] - 1 + 127 - 7, 1), 1, 254)
    codes = (v * np.exp2(127.0 - byte)[:, None, :]).reshape(n, m).astype(np.float32).astype(ml_dtypes.float8_e4m3fn).view(np.uint8)
    words = codes.reshape(n // 512, 128, 4, m).transpose(0, 1, 3, 2)
    return np.ascontiguousarray(words), np.ascontiguousarray(byte.astype(np.uint8).reshape(n // 512, 16, m))


K, T, S, N, H, W = 512, 2048, 512, 512, 512, 256


def setup_inputs():
    n = np.random.standard_normal
    s = mx_kscale(K)[:, None]
    u = mx_kscale(H)
    packed_xT = pack_weight(n((K, T)) * s)
    packed_w1 = pack_fp4(n((K, H)) / np.sqrt(K) / s)
    packed_w2 = pack_fp4(n((H, N)) / np.sqrt(H) / u[:, None])
    perm = np.stack([np.random.permutation(S) for _ in range(8)])
    return {
        "x_words": packed_xT[0],
        "x_scales": packed_xT[1],
        "w1_words": packed_w1[0],
        "w1_scales": packed_w1[1],
        "gn": (np.random.uniform(0.5, 1.5, (H, 1)) * u[:, None]).astype(np.float32),
        "w2_words": packed_w2[0],
        "w2_scales": packed_w2[1],
        "offs": striped(np.random.permutation(T)[:S]),
        "n1": striped8(perm[:, :W]),
        "n2": striped8(perm[:, W:]),
        "n3": striped8(np.stack([np.random.permutation(S) for _ in range(8)])),
        "n4": striped8(np.stack([np.random.permutation(S) for _ in range(8)])),
    }


def reference(x_words, x_scales, w1_words, w1_scales, gn, w2_words, w2_scales, offs, n1, n2, n3, n4):
    xq = unpack_weight(x_words, x_scales)[:, unstriped(offs)]
    y = unpack_fp4(w1_words, w1_scales).T @ xq
    pb = y[np.arange(H)[:, None], runs(n2, H)]
    pa = y[np.arange(H)[:, None], runs(n1, H)]
    rb = pb - (0.5 * pa)
    ra = np.sqrt((pa) ** 2 + (pb) ** 2 + 0.25)
    ds = np.zeros((H, S))
    ds[np.arange(H)[:, None], runs(n1, H)] = ra
    dt = ds.copy()
    dt[np.arange(H)[:, None], runs(n2, H)] = rb
    z = f64(gn) * dt
    h = unpack_fp4(w2_words, w2_scales).T @ mxq(z, 0, "e4m3")
    st = h + 0.5 * (h[np.arange(N)[:, None], runs(n3, N)])
    out_0 = st - (st[np.arange(N)[:, None], runs(n4, N)])
    return (out_0,) + planes(out_0)

@@ -1,0 +1,226 @@
+from contextlib import ExitStack
+
+import concourse.mybir as mybir
+
+F32 = mybir.dt.float32
+BF16 = mybir.dt.bfloat16
+I32 = mybir.dt.int32
+U32 = mybir.dt.uint32
+U16 = mybir.dt.uint16
+U8 = mybir.dt.uint8
+FP8X4 = mybir.dt.float8_e4m3fn_x4
+FP4X4 = mybir.dt.float4_e2m1fn_x4
+ALU = mybir.AluOpType
+ACT = mybir.ActivationFunctionType
+
+P = 128
+PACK = 4
+T = 2048
+S = 512
+W = 256
+HALF = S // 2
+OUT_CHUNKS = ((0, 256), (256, 384), (384, 512))
+
+FLOPS = 2 * 2 * 512 * 512 * 512
+
+
+def entries(lst, a, b):
+    return lst[:, a // 16 : b // 16]
+
+
+def tile_picked_laypolarhop_none_po_kernel(
+    tc, x_words, x_scales, w1_words, w1_scales, gn, w2_words, w2_scales, offs, n1, n2, n3, n4, out_0, out_1, out_2
+):
+    nc = tc.nc
+    with ExitStack() as ctx:
+        sb = ctx.enter_context(tc.tile_pool(name="sb", bufs=1))
+        psum = ctx.enter_context(tc.psum_pool(name="psum", bufs=8))
+
+        offs_t = sb.tile([P, S // 16], U16, name="offs_t")
+        n1_t = sb.tile([P, W // 16], U16, name="n1_t")
+        n2_t = sb.tile([P, W // 16], U16, name="n2_t")
+        n3_t = sb.tile([P, S // 16], U16, name="n3_t")
+        n4_t = sb.tile([P, S // 16], U16, name="n4_t")
+
+        xw = sb.tile([P, T], U32, name="xw", align_bytes=64)
+        xs = sb.tile([P, T], U8, name="xs", align_bytes=64)
+        w1_raw = sb.tile([P, 2 * S], U8, name="w1_raw", align_bytes=64)
+        w2_raw = sb.tile([P, 2 * S], U8, name="w2_raw", align_bytes=64)
+        s1_raw = sb.tile([P, S], U8, name="s1_raw", align_bytes=64)
+        s2_raw = sb.tile([P, S], U8, name="s2_raw", align_bytes=64)
+        gain = sb.tile([P, PACK], F32, name="gain")
+
+        def load_scales(tile, rows, quadrants):
+            for q in quadrants:
+                src = rows[0, 4 * q : 4 * q + 4, :].bitcast(I32)
+                nc.sync.dma_start(out=tile[32 * q : 32 * q + 32, :].bitcast(I32), in_=src.unsqueeze(0).to_broadcast([8, 4, src.shape[1]]))
+
+        nc.sync.dma_start(out=w1_raw[:].bitcast(I32), in_=w1_words[0].bitcast(I32))
+        nc.sync.dma_start(out=offs_t[:], in_=offs)
+        load_scales(xs, x_scales, range(4))
+        load_scales(s1_raw, w1_scales, range(1))
+        nc.sync.dma_start(out=xw[:].bitcast(I32), in_=x_words[0].rearrange("p c r -> p (c r)").bitcast(I32))
+        load_scales(s1_raw, w1_scales, range(1, 4))
+        nc.sync.dma_start(out=n1_t[:], in_=n1)
+        nc.sync.dma_start(out=n2_t[:], in_=n2)
+        nc.sync.dma_start(out=w2_raw[:].bitcast(I32), in_=w2_words[0].bitcast(I32))
+        nc.sync.dma_start(out=gain[:], in_=gn.rearrange("(p t) o -> p (t o)", t=PACK))
+        load_scales(s2_raw, w2_scales, range(4))
+        nc.sync.dma_start(out=n3_t[:], in_=n3)
+        nc.sync.dma_start(out=n4_t[:], in_=n4)
+        warm = sb.tile([P, 1], F32, name="warm")
+        nc.vector.memset(warm[:], 1.0)
+        nc.scalar.activation(out=warm[:], in_=warm[:], func=ACT.Sqrt, bias=0.25)
+
+        def deal_words(raw, name, t0, t1, tag):
+            dealt = sb.tile([P, t1 - t0, P, 2], U8, name=name, tag=tag, align_bytes=64)
+            nc.vector.tensor_copy(out=dealt[:], in_=raw[:].rearrange("p (m t b) -> p t m b", t=PACK, b=2)[:, t0:t1])
+            return [dealt[:, t].rearrange("p m b -> p (m b)") for t in range(t1 - t0)]
+
+        def deal_scales(raw, name, t0, t1, tag):
+            dealt = sb.tile([P, t1 - t0, P], U8, name=name, tag=tag, align_bytes=64)
+            nc.vector.tensor_copy(out=dealt[:], in_=raw[:].rearrange("p (m t) -> p t m", t=PACK)[:, t0:t1])
+            return [dealt[:, t] for t in range(t1 - t0)]
+
+        def product(acc, words, scales, codes, code_scales):
+            nc.tensor.matmul_mx(out=acc, lhsT=words.bitcast(FP4X4), lhsT_scale=scales, rhs=codes.bitcast(FP8X4), rhs_scale=code_scales, start=True, stop=True)
+
+        w1 = deal_words(w1_raw, "w1_all", 0, 4, "w1_all")
+        gs = sb.tile([P, S], U8, name="gs", align_bytes=64)
+        nc.vector.tensor_copy(out=gs[:], in_=xs[:].indirect(offs_t[:]))
+        gw = sb.tile([P, S], U32, name="gw", align_bytes=64)
+        y = [sb.tile([P, S], F32, name="y%d" % t, tag="y%d" % t, align_bytes=64) for t in range(PACK)]
+        for a in (0, HALF):
+            cols = slice(a, a + HALF)
+            nc.vector.tensor_copy(out=gw[:, cols], in_=xw[:].indirect(entries(offs_t, a, a + HALF)))
+            if a == 0:
+                s1 = deal_scales(s1_raw, "s1_first", 0, 1, "s1_first")
+            acc = psum.tile([P, S], F32, name="acc")
+            product(acc[:, :HALF], w1[0], s1[0], gw[:, cols], gs[:, cols])
+            nc.scalar.copy(out=y[0][:, cols], in_=acc[:, :HALF])
+        s1 = s1 + deal_scales(s1_raw, "s1_rest", 1, 4, "s1_rest")
+        for t in range(1, PACK):
+            acc = psum.tile([P, S], F32, name="acc")
+            product(acc[:], w1[t], s1[t], gw[:], gs[:])
+            nc.scalar.copy(out=y[t][:], in_=acc[:])
+
+
+        pair = [sb.tile([P, 2 * W], F32, name="pair%d" % t) for t in range(PACK)]
+        win = [sb.tile([P, 2 * S], F32, name="win%d" % t) for t in range(PACK)]
+        squares = [win[t][:, S:] for t in range(PACK)]
+        total = [sb.tile([P, W], F32, name="total%d" % t) for t in range(PACK)]
+        ra = [sb.tile([P, W], F32, name="ra%d" % t) for t in range(PACK)]
+        dt = [sb.tile([P, S], F32, name="dt%d" % t) for t in range(PACK)]
+        z = [sb.tile([P, HALF, PACK], BF16, name="z%d" % h, tag="z%d" % h, align_bytes=64) for h in range(2)]
+
+        def fetch(t):
+            nc.vector.tensor_scalar(out=pair[t][:, :W], in0=y[t][:].indirect(n1_t[:]), scalar1=-0.5, scalar2=0.0, op0=ALU.mult, op1=ALU.add)
+            nc.vector.tensor_copy(out=pair[t][:, W:], in_=y[t][:].indirect(n2_t[:]))
+            nc.scalar.activation(out=squares[t][:, :W], in_=pair[t][:, :W], func=ACT.Square, scale=2.0)
+            nc.scalar.activation(out=squares[t][:, W:], in_=pair[t][:, W:], func=ACT.Square)
+
+        def put_rb(t):
+            nc.vector.tensor_tensor(out=dt[t][:].indirect(n2_t[:]), in0=pair[t][:, W:], in1=pair[t][:, :W], op=ALU.add)
+
+        def root(t):
+            nc.gpsimd.tensor_tensor(out=total[t][:], in0=squares[t][:, :W], in1=squares[t][:, W:], op=ALU.add)
+            nc.scalar.activation(out=ra[t][:], in_=total[t][:], func=ACT.Sqrt, bias=0.25)
+
+        def put_ra(t):
+            nc.vector.tensor_copy(out=dt[t][:].indirect(n1_t[:]), in_=ra[t][:])
+            for h in range(2):
+                src = dt[t][:, h * HALF : (h + 1) * HALF]
+                if h == 1 and t >= 2:
+                    nc.vector.tensor_scalar(out=z[h][:, :, t], in0=src, scalar1=gain[:, t : t + 1], scalar2=None, op0=ALU.mult)
+                else:
+                    nc.scalar.activation(out=z[h][:, :, t], in_=src, func=ACT.Copy, scale=gain[:, t : t + 1])
+
+        fetch(0)
+        for t in range(PACK):
+            root(t)
+            put_rb(t)
+            if t + 1 < PACK:
+                fetch(t + 1)
+            if t == 2:
+                w2 = deal_words(w2_raw, "w2_first", 0, 1, "y1")
+                s2 = deal_scales(s2_raw, "s2_first", 0, 1, "y2")
+            put_ra(t)
+
+        zq = [sb.tile([P, HALF], U32, name="zq%d" % h, align_bytes=64) for h in range(2)]
+        zs = [sb.tile([P, HALF], U8, name="zs%d" % h, align_bytes=64) for h in range(2)]
+        hh = [sb.tile([P, S], F32, name="hh%d" % t) for t in range(PACK)]
+        for h in (1, 0):
+            nc.vector.quantize_mx(out=zq[h][:].bitcast(FP8X4), scales=zs[h][:], in_=z[h][:].rearrange("p c t -> p (c t)"))
+            cols = slice(h * HALF, (h + 1) * HALF)
+            acc = psum.tile([P, S], F32, name="acc")
+            product(acc[:, :HALF], w2[0], s2[0], zq[h][:], zs[h][:])
+            nc.scalar.activation(out=win[0][:, cols], in_=acc[:, :HALF], func=ACT.Copy, scale=-0.5)
+            nc.scalar.copy(out=hh[0][:, cols], in_=acc[:, :HALF])
+
+        s2 = s2 + deal_scales(s2_raw, "s2_rest", 1, 4, "z1")
+        w2 = w2 + deal_words(w2_raw, "w2_rest", 1, 4, "z0")
+
+        def second_layer(t):
+            acc = psum.tile([P, S], F32, name="acc")
+            for h in (1, 0):
+                product(acc[:, h * HALF : (h + 1) * HALF], w2[t], s2[t], zq[h][:], zs[h][:])
+            nc.scalar.activation(out=win[t][:, :S], in_=acc[:], func=ACT.Copy, scale=-0.5)
+            nc.scalar.copy(out=hh[t][:], in_=acc[:])
+
+        neg_st = [sb.tile([P, S], F32, name="neg_st%d" % t) for t in range(PACK)]
+        neg_st_copy = [sb.tile([P, S], F32, name="neg_st_copy%d" % t) for t in range(PACK)]
+
+        def first_hop(t):
+            for a, b in ((HALF, S), (0, HALF)) if t == 0 else ((0, S),):
+                nc.vector.tensor_tensor(out=neg_st[t][:, a:b], in0=win[t][:].indirect(entries(n3_t, a, b)), in1=hh[t][:, a:b], op=ALU.subtract)
+
+        res = [sb.tile([P, PACK, b - a], F32, name="res%d" % a) for a, b in OUT_CHUNKS]
+        out_scales = sb.tile([P, S], U8, name="out_scales", align_bytes=64)
+        out_rows = out_0.rearrange("(p t) j -> p t j", t=PACK)
+        out_words = out_1[0].rearrange("p c r -> p (c r)").bitcast(I32)
+
+        def copy_st(t, a, b):
+            nc.scalar.copy(out=neg_st_copy[t][:, a:b], in_=neg_st[t][:, a:b])
+
+        def second_hop(c, t):
+            a, b = OUT_CHUNKS[c]
+            nc.vector.tensor_tensor(out=res[c][:, t, :], in0=neg_st[t][:].indirect(entries(n4_t, a, b)), in1=neg_st_copy[t][:, a:b], op=ALU.subtract)
+
+        def regroup(c, copy):
+            a, b = OUT_CHUNKS[c]
+            nc.sync.dma_start(out=out_rows[:, :, a:b], in_=res[c][:])
+            grouped = sb.tile([P, b - a, PACK], BF16, name="grouped%d" % c, align_bytes=64)
+            copy(out=grouped[:].rearrange("p (c i) t -> p c t i", i=4), in_=res[c][:].rearrange("p t (c i) -> p c t i", i=4))
+            return grouped
+
+        def quantise_out(c, grouped):
+            a, b = OUT_CHUNKS[c]
+            codes = sb.tile([P, b - a], U32, name="codes%d" % c, align_bytes=64)
+            nc.vector.quantize_mx(out=codes[:].bitcast(FP8X4), scales=out_scales[:, a:b], in_=grouped[:].rearrange("p c t -> p (c t)"))
+            nc.sync.dma_start(out=out_words[:, a:b], in_=codes[:].bitcast(I32))
+
+        second_layer(1)
+        first_hop(0)
+        copy_st(0, 0, HALF)
+        for t in range(1, PACK):
+            if t + 1 < PACK:
+                second_layer(t + 1)
+            first_hop(t)
+            copy_st(t, 0, HALF)
+            second_hop(0, t - 1)
+        second_hop(0, PACK - 1)
+        for t in range(PACK):
+            copy_st(t, HALF, S)
+        g0 = regroup(0, nc.scalar.copy)
+        for t in range(PACK):
+            second_hop(1, t)
+        quantise_out(0, g0)
+        g1 = regroup(1, nc.scalar.copy)
+        for t in range(PACK):
+            second_hop(2, t)
+        quantise_out(1, g1)
+        g2 = regroup(2, nc.vector.tensor_copy)
+        quantise_out(2, g2)
+        for q in range(4):
+            engine = nc.scalar if q % 2 else nc.sync
+            engine.dma_start(out=out_2[0, 4 * q : 4 * q + 4, :].bitcast(I32), in_=out_scales[32 * q : 32 * q + 4, :].bitcast(I32))

@@ -1,6 +1,7 @@
 from contextlib import ExitStack
 
 import concourse.mybir as mybir
+from concourse.masks import make_identity
 
 F32 = mybir.dt.float32
 BF16 = mybir.dt.bfloat16
@@ -34,6 +35,8 @@ def tile_picked_laypolarhop_none_po_kernel(
     nc = tc.nc
     with ExitStack() as ctx:
         sb = ctx.enter_context(tc.tile_pool(name="sb", bufs=1))
+        relay = ctx.enter_context(tc.tile_pool(name="relay", bufs=1))
+        table = ctx.enter_context(tc.tile_pool(name="table", bufs=1))
         psum = ctx.enter_context(tc.psum_pool(name="psum", bufs=8))
 
         offs_t = sb.tile([P, S // 16], U16, name="offs_t")
@@ -42,7 +45,7 @@ def tile_picked_laypolarhop_none_po_kernel(
         n3_t = sb.tile([P, S // 16], U16, name="n3_t")
         n4_t = sb.tile([P, S // 16], U16, name="n4_t")
 
-        xw = sb.tile([P, T], U32, name="xw", align_bytes=64)
+        xw = table.tile([P, T], U32, name="xw", align_bytes=64, offset=0)
         xs = sb.tile([P, T], U8, name="xs", align_bytes=64)
         w1_raw = sb.tile([P, 2 * S], U8, name="w1_raw", align_bytes=64)
         w2_raw = sb.tile([P, 2 * S], U8, name="w2_raw", align_bytes=64)
@@ -50,55 +53,58 @@ def tile_picked_laypolarhop_none_po_kernel(
         s2_raw = sb.tile([P, S], U8, name="s2_raw", align_bytes=64)
         gain = sb.tile([P, PACK], F32, name="gain")
 
-        def load_scales(tile, rows, quadrants):
+        def load_scales(engine, tile, rows, quadrants):
             for q in quadrants:
                 src = rows[0, 4 * q : 4 * q + 4, :].bitcast(I32)
-                nc.sync.dma_start(out=tile[32 * q : 32 * q + 32, :].bitcast(I32), in_=src.unsqueeze(0).to_broadcast([8, 4, src.shape[1]]))
+                engine.dma_start(out=tile[32 * q : 32 * q + 32, :].bitcast(I32), in_=src.unsqueeze(0).to_broadcast([8, 4, src.shape[1]]))
 
         nc.sync.dma_start(out=w1_raw[:].bitcast(I32), in_=w1_words[0].bitcast(I32))
         nc.sync.dma_start(out=offs_t[:], in_=offs)
-        load_scales(xs, x_scales, range(4))
-        load_scales(s1_raw, w1_scales, range(1))
+        load_scales(nc.sync, xs, x_scales, range(4))
+        load_scales(nc.sync, s1_raw, w1_scales, range(1))
         nc.sync.dma_start(out=xw[:].bitcast(I32), in_=x_words[0].rearrange("p c r -> p (c r)").bitcast(I32))
-        load_scales(s1_raw, w1_scales, range(1, 4))
+        load_scales(nc.sync, s1_raw, w1_scales, range(1, 4))
         nc.sync.dma_start(out=n1_t[:], in_=n1)
         nc.sync.dma_start(out=n2_t[:], in_=n2)
         nc.sync.dma_start(out=w2_raw[:].bitcast(I32), in_=w2_words[0].bitcast(I32))
         nc.sync.dma_start(out=gain[:], in_=gn.rearrange("(p t) o -> p (t o)", t=PACK))
-        load_scales(s2_raw, w2_scales, range(4))
+        load_scales(nc.gpsimd, s2_raw, w2_scales, range(4))
         nc.sync.dma_start(out=n3_t[:], in_=n3)
         nc.sync.dma_start(out=n4_t[:], in_=n4)
         warm = sb.tile([P, 1], F32, name="warm")
         nc.vector.memset(warm[:], 1.0)
         nc.scalar.activation(out=warm[:], in_=warm[:], func=ACT.Sqrt, bias=0.25)
 
-        def deal_words(raw, name, t0, t1, tag):
-            dealt = sb.tile([P, t1 - t0, P, 2], U8, name=name, tag=tag, align_bytes=64)
-            nc.vector.tensor_copy(out=dealt[:], in_=raw[:].rearrange("p (m t b) -> p t m b", t=PACK, b=2)[:, t0:t1])
-            return [dealt[:, t].rearrange("p m b -> p (m b)") for t in range(t1 - t0)]
+        ident = sb.tile([P, P], F32, name="ident")
+        make_identity(nc, ident[:])
 
-        def deal_scales(raw, name, t0, t1, tag):
-            dealt = sb.tile([P, t1 - t0, P], U8, name=name, tag=tag, align_bytes=64)
-            nc.vector.tensor_copy(out=dealt[:], in_=raw[:].rearrange("p (m t) -> p t m", t=PACK)[:, t0:t1])
-            return [dealt[:, t] for t in range(t1 - t0)]
+        def deal_words(raw, dealt):
+            nc.vector.tensor_copy(out=dealt[:], in_=raw[:].rearrange("p (m t b) -> p t m b", t=PACK, b=2))
+            return [dealt[:, t].rearrange("p m b -> p (m b)") for t in range(PACK)]
+
+        def deal_scales(raw, dealt):
+            nc.vector.tensor_copy(out=dealt[:], in_=raw[:].rearrange("p (m t) -> p t m", t=PACK))
+            return [dealt[:, t] for t in range(PACK)]
 
         def product(acc, words, scales, codes, code_scales):
             nc.tensor.matmul_mx(out=acc, lhsT=words.bitcast(FP4X4), lhsT_scale=scales, rhs=codes.bitcast(FP8X4), rhs_scale=code_scales, start=True, stop=True)
 
-        w1 = deal_words(w1_raw, "w1_all", 0, 4, "w1_all")
+        w1 = deal_words(w1_raw, sb.tile([P, PACK, P, 2], U8, name="w1_dealt", align_bytes=64))
         gs = sb.tile([P, S], U8, name="gs", align_bytes=64)
         nc.vector.tensor_copy(out=gs[:], in_=xs[:].indirect(offs_t[:]))
         gw = sb.tile([P, S], U32, name="gw", align_bytes=64)
-        y = [sb.tile([P, S], F32, name="y%d" % t, tag="y%d" % t, align_bytes=64) for t in range(PACK)]
+        y = [sb.tile([P, S], F32, name="y%d" % t, tag="y%d" % t, align_bytes=64) for t in range(PACK - 1)]
+        y.append(relay.tile([P, S], F32, name="y3", offset=1024))
         for a in (0, HALF):
             cols = slice(a, a + HALF)
             nc.vector.tensor_copy(out=gw[:, cols], in_=xw[:].indirect(entries(offs_t, a, a + HALF)))
             if a == 0:
-                s1 = deal_scales(s1_raw, "s1_first", 0, 1, "s1_first")
+                s1 = deal_scales(s1_raw, sb.tile([P, PACK, P], U8, name="s1_dealt", align_bytes=64))
             acc = psum.tile([P, S], F32, name="acc")
             product(acc[:, :HALF], w1[0], s1[0], gw[:, cols], gs[:, cols])
             nc.scalar.copy(out=y[0][:, cols], in_=acc[:, :HALF])
-        s1 = s1 + deal_scales(s1_raw, "s1_rest", 1, 4, "s1_rest")
+        w2 = deal_words(w2_raw, table.tile([P, PACK, P, 2], U8, name="w2_dealt", align_bytes=64, offset=0))
+        s2 = deal_scales(s2_raw, table.tile([P, PACK, P], U8, name="s2_dealt", align_bytes=64, offset=2 * S))
         for t in range(1, PACK):
             acc = psum.tile([P, S], F32, name="acc")
             product(acc[:], w1[t], s1[t], gw[:], gs[:])
@@ -108,10 +114,9 @@ def tile_picked_laypolarhop_none_po_kernel(
         pair = [sb.tile([P, 2 * W], F32, name="pair%d" % t) for t in range(PACK)]
         win = [sb.tile([P, 2 * S], F32, name="win%d" % t) for t in range(PACK)]
         squares = [win[t][:, S:] for t in range(PACK)]
-        total = [sb.tile([P, W], F32, name="total%d" % t) for t in range(PACK)]
-        ra = [sb.tile([P, W], F32, name="ra%d" % t) for t in range(PACK)]
-        dt = [sb.tile([P, S], F32, name="dt%d" % t) for t in range(PACK)]
-        z = [sb.tile([P, HALF, PACK], BF16, name="z%d" % h, tag="z%d" % h, align_bytes=64) for h in range(2)]
+        turned = [sb.tile([P, W], F32, name="turned%d" % t, tag="turned%d" % t, align_bytes=64) for t in range(PACK)]
+        dt = [relay.tile([P, S], F32, name="dt%d" % t, offset=2048 * t) for t in range(2)]
+        dt.extend(sb.tile([P, S], F32, name="dt%d" % t, tag="dt%d" % t, align_bytes=64) for t in range(2, PACK))
 
         def fetch(t):
             nc.vector.tensor_scalar(out=pair[t][:, :W], in0=y[t][:].indirect(n1_t[:]), scalar1=-0.5, scalar2=0.0, op0=ALU.mult, op1=ALU.add)
@@ -123,11 +128,27 @@ def tile_picked_laypolarhop_none_po_kernel(
             nc.vector.tensor_tensor(out=dt[t][:].indirect(n2_t[:]), in0=pair[t][:, W:], in1=pair[t][:, :W], op=ALU.add)
 
         def root(t):
-            nc.gpsimd.tensor_tensor(out=total[t][:], in0=squares[t][:, :W], in1=squares[t][:, W:], op=ALU.add)
-            nc.scalar.activation(out=ra[t][:], in_=total[t][:], func=ACT.Sqrt, bias=0.25)
+            total = psum.tile([P, S], F32, name="acc")
+            for a in (0, P):
+                for u in range(2):
+                    nc.tensor.matmul(out=total[:, a : a + P], lhsT=squares[t][:, u * W + a : u * W + a + P], rhs=ident[:], is_transpose=True, start=(u == 0), stop=(u == 1))
+            nc.scalar.activation(out=turned[t][:], in_=total[:, :W], func=ACT.Sqrt, bias=0.25)
+            back = psum.tile([P, S], F32, name="acc")
+            for a in (0, P):
+                nc.tensor.transpose(back[:, a : a + P], turned[t][:, a : a + P], ident[:])
+            nc.scalar.copy(out=ra[:, t, :], in_=back[:, :W])
 
-        def put_ra(t):
-            nc.vector.tensor_copy(out=dt[t][:].indirect(n1_t[:]), in_=ra[t][:])
+        ra = sb.tile([P, PACK, W], F32, name="ra")
+        for t in range(PACK):
+            fetch(t)
+        for t in range(PACK):
+            root(t)
+        for t in range(PACK):
+            put_rb(t)
+        z_all = sb.tile([P, 2, HALF, PACK], BF16, name="z_all", tag="turned3", align_bytes=64)
+        z = [z_all[:, h] for h in range(2)]
+        for t in range(PACK):
+            nc.vector.tensor_copy(out=dt[t][:].indirect(n1_t[:]), in_=ra[:, t, :])
             for h in range(2):
                 src = dt[t][:, h * HALF : (h + 1) * HALF]
                 if h == 1 and t >= 2:
@@ -135,30 +156,17 @@ def tile_picked_laypolarhop_none_po_kernel(
                 else:
                     nc.scalar.activation(out=z[h][:, :, t], in_=src, func=ACT.Copy, scale=gain[:, t : t + 1])
 
-        fetch(0)
-        for t in range(PACK):
-            root(t)
-            put_rb(t)
-            if t + 1 < PACK:
-                fetch(t + 1)
-            if t == 2:
-                w2 = deal_words(w2_raw, "w2_first", 0, 1, "y1")
-                s2 = deal_scales(s2_raw, "s2_first", 0, 1, "y2")
-            put_ra(t)
-
         zq = [sb.tile([P, HALF], U32, name="zq%d" % h, align_bytes=64) for h in range(2)]
         zs = [sb.tile([P, HALF], U8, name="zs%d" % h, align_bytes=64) for h in range(2)]
         hh = [sb.tile([P, S], F32, name="hh%d" % t) for t in range(PACK)]
         for h in (1, 0):
-            nc.vector.quantize_mx(out=zq[h][:].bitcast(FP8X4), scales=zs[h][:], in_=z[h][:].rearrange("p c t -> p (c t)"))
+            nc.vector.quantize_mx(out=zq[h][:].bitcast(FP8X4), scales=zs[h][:], in_=z[h].rearrange("p c t -> p (c t)"))
             cols = slice(h * HALF, (h + 1) * HALF)
             acc = psum.tile([P, S], F32, name="acc")
             product(acc[:, :HALF], w2[0], s2[0], zq[h][:], zs[h][:])
             nc.scalar.activation(out=win[0][:, cols], in_=acc[:, :HALF], func=ACT.Copy, scale=-0.5)
-            nc.scalar.copy(out=hh[0][:, cols], in_=acc[:, :HALF])
+            (nc.vector.tensor_copy if h else nc.scalar.copy)(out=hh[0][:, cols], in_=acc[:, :HALF])
 
-        s2 = s2 + deal_scales(s2_raw, "s2_rest", 1, 4, "z1")
-        w2 = w2 + deal_words(w2_raw, "w2_rest", 1, 4, "z0")
 
         def second_layer(t):
             acc = psum.tile([P, S], F32, name="acc")
@@ -168,29 +176,30 @@ def tile_picked_laypolarhop_none_po_kernel(
             nc.scalar.copy(out=hh[t][:], in_=acc[:])
 
         neg_st = [sb.tile([P, S], F32, name="neg_st%d" % t) for t in range(PACK)]
-        neg_st_copy = [sb.tile([P, S], F32, name="neg_st_copy%d" % t) for t in range(PACK)]
+        copies = [sb.tile([P, PACK, HALF], F32, name="copies%d" % h, tag="copies%d" % h, align_bytes=64) for h in range(2)]
 
         def first_hop(t):
             for a, b in ((HALF, S), (0, HALF)) if t == 0 else ((0, S),):
                 nc.vector.tensor_tensor(out=neg_st[t][:, a:b], in0=win[t][:].indirect(entries(n3_t, a, b)), in1=hh[t][:, a:b], op=ALU.subtract)
 
-        res = [sb.tile([P, PACK, b - a], F32, name="res%d" % a) for a, b in OUT_CHUNKS]
+        res_first = sb.tile([P, PACK, HALF], F32, name="res_first")
+        res = [res_first[:]]
         out_scales = sb.tile([P, S], U8, name="out_scales", align_bytes=64)
         out_rows = out_0.rearrange("(p t) j -> p t j", t=PACK)
         out_words = out_1[0].rearrange("p c r -> p (c r)").bitcast(I32)
 
         def copy_st(t, a, b):
-            nc.scalar.copy(out=neg_st_copy[t][:, a:b], in_=neg_st[t][:, a:b])
+            nc.scalar.copy(out=copies[a // HALF][:, t, :], in_=neg_st[t][:, a:b])
 
         def second_hop(c, t):
             a, b = OUT_CHUNKS[c]
-            nc.vector.tensor_tensor(out=res[c][:, t, :], in0=neg_st[t][:].indirect(entries(n4_t, a, b)), in1=neg_st_copy[t][:, a:b], op=ALU.subtract)
+            nc.vector.tensor_tensor(out=res[c][:, t, :], in0=neg_st[t][:].indirect(entries(n4_t, a, b)), in1=copies[a // HALF][:, t, a % HALF : a % HALF + b - a], op=ALU.subtract)
 
         def regroup(c, copy):
             a, b = OUT_CHUNKS[c]
-            nc.sync.dma_start(out=out_rows[:, :, a:b], in_=res[c][:])
+            nc.sync.dma_start(out=out_rows[:, :, a:b], in_=res[c])
             grouped = sb.tile([P, b - a, PACK], BF16, name="grouped%d" % c, align_bytes=64)
-            copy(out=grouped[:].rearrange("p (c i) t -> p c t i", i=4), in_=res[c][:].rearrange("p t (c i) -> p c t i", i=4))
+            copy(out=grouped[:].rearrange("p (c i) t -> p c t i", i=4), in_=res[c].rearrange("p t (c i) -> p c t i", i=4))
             return grouped
 
         def quantise_out(c, grouped):
@@ -211,6 +220,8 @@ def tile_picked_laypolarhop_none_po_kernel(
         second_hop(0, PACK - 1)
         for t in range(PACK):
             copy_st(t, HALF, S)
+        res_rest = sb.tile([P, 2, PACK, P], F32, name="res_rest", tag="copies0", align_bytes=64)
+        res.extend([res_rest[:, 0], res_rest[:, 1]])
         g0 = regroup(0, nc.scalar.copy)
         for t in range(PACK):
             second_hop(1, t)

@@ -45,11 +45,11 @@ def tile_picked_laypolarhop_none_po_kernel(
         n3_t = sb.tile([P, S // 16], U16, name="n3_t")
         n4_t = sb.tile([P, S // 16], U16, name="n4_t")
 
-        xw = table.tile([P, T], U32, name="xw", align_bytes=64, offset=0)
+        xw = table.tile([P, T], U32, name="xw", align_bytes=64, offset=S)
         xs = sb.tile([P, T], U8, name="xs", align_bytes=64)
         w1_raw = sb.tile([P, 2 * S], U8, name="w1_raw", align_bytes=64)
-        w2_raw = sb.tile([P, 2 * S], U8, name="w2_raw", align_bytes=64)
-        s1_raw = sb.tile([P, S], U8, name="s1_raw", align_bytes=64)
+        w2_raw = sb.tile([P, 2 * S], U8, name="w2_raw", tag="pair0", align_bytes=64)
+        s1_raw = table.tile([P, S], U8, name="s1_raw", align_bytes=64, offset=0)
         s2_raw = sb.tile([P, S], U8, name="s2_raw", align_bytes=64)
         gain = sb.tile([P, PACK], F32, name="gain")
 
@@ -64,11 +64,11 @@ def tile_picked_laypolarhop_none_po_kernel(
         load_scales(nc.sync, s1_raw, w1_scales, range(1))
         nc.sync.dma_start(out=xw[:].bitcast(I32), in_=x_words[0].rearrange("p c r -> p (c r)").bitcast(I32))
         load_scales(nc.sync, s1_raw, w1_scales, range(1, 4))
+        nc.sync.dma_start(out=w2_raw[:].bitcast(I32), in_=w2_words[0].bitcast(I32))
         nc.sync.dma_start(out=n1_t[:], in_=n1)
         nc.sync.dma_start(out=n2_t[:], in_=n2)
-        nc.sync.dma_start(out=w2_raw[:].bitcast(I32), in_=w2_words[0].bitcast(I32))
         nc.sync.dma_start(out=gain[:], in_=gn.rearrange("(p t) o -> p (t o)", t=PACK))
-        load_scales(nc.gpsimd, s2_raw, w2_scales, range(4))
+        load_scales(nc.sync, s2_raw, w2_scales, range(4))
         nc.sync.dma_start(out=n3_t[:], in_=n3)
         nc.sync.dma_start(out=n4_t[:], in_=n4)
         warm = sb.tile([P, 1], F32, name="warm")
@@ -104,14 +104,13 @@ def tile_picked_laypolarhop_none_po_kernel(
             product(acc[:, :HALF], w1[0], s1[0], gw[:, cols], gs[:, cols])
             nc.scalar.copy(out=y[0][:, cols], in_=acc[:, :HALF])
         w2 = deal_words(w2_raw, table.tile([P, PACK, P, 2], U8, name="w2_dealt", align_bytes=64, offset=0))
-        s2 = deal_scales(s2_raw, table.tile([P, PACK, P], U8, name="s2_dealt", align_bytes=64, offset=2 * S))
         for t in range(1, PACK):
             acc = psum.tile([P, S], F32, name="acc")
             product(acc[:], w1[t], s1[t], gw[:], gs[:])
             nc.scalar.copy(out=y[t][:], in_=acc[:])
 
 
-        pair = [sb.tile([P, 2 * W], F32, name="pair%d" % t) for t in range(PACK)]
+        pair = [sb.tile([P, 2 * W], F32, name="pair%d" % t, tag="pair%d" % t, align_bytes=64) for t in range(PACK)]
         win = [sb.tile([P, 2 * S], F32, name="win%d" % t) for t in range(PACK)]
         squares = [win[t][:, S:] for t in range(PACK)]
         turned = [sb.tile([P, W], F32, name="turned%d" % t, tag="turned%d" % t, align_bytes=64) for t in range(PACK)]
@@ -139,12 +138,14 @@ def tile_picked_laypolarhop_none_po_kernel(
             nc.scalar.copy(out=ra[:, t, :], in_=back[:, :W])
 
         ra = sb.tile([P, PACK, W], F32, name="ra")
+        fetch(0)
         for t in range(PACK):
-            fetch(t)
-        for t in range(PACK):
+            if t + 1 < PACK:
+                fetch(t + 1)
             root(t)
         for t in range(PACK):
             put_rb(t)
+        s2 = deal_scales(s2_raw, sb.tile([P, PACK, P], U8, name="s2_dealt", tag="y2", align_bytes=64))
         z_all = sb.tile([P, 2, HALF, PACK], BF16, name="z_all", tag="turned3", align_bytes=64)
         z = [z_all[:, h] for h in range(2)]
         for t in range(PACK):

@@ -71,9 +71,6 @@ def tile_picked_laypolarhop_none_po_kernel(
         load_scales(nc.sync, s2_raw, w2_scales, range(4))
         nc.sync.dma_start(out=n3_t[:], in_=n3)
         nc.sync.dma_start(out=n4_t[:], in_=n4)
-        warm = sb.tile([P, 1], F32, name="warm")
-        nc.vector.memset(warm[:], 1.0)
-        nc.scalar.activation(out=warm[:], in_=warm[:], func=ACT.Sqrt, bias=0.25)
 
         ident = sb.tile([P, P], F32, name="ident")
         make_identity(nc, ident[:])

from contextlib import ExitStack

import concourse.mybir as mybir
from concourse.masks import make_identity

F32 = mybir.dt.float32
BF16 = mybir.dt.bfloat16
I32 = mybir.dt.int32
U32 = mybir.dt.uint32
U16 = mybir.dt.uint16
U8 = mybir.dt.uint8
FP8X4 = mybir.dt.float8_e4m3fn_x4
FP4X4 = mybir.dt.float4_e2m1fn_x4
ALU = mybir.AluOpType
ACT = mybir.ActivationFunctionType

P = 128
PACK = 4
T = 2048
S = 512
W = 256
HALF = S // 2
OUT_CHUNKS = ((0, 256), (256, 384), (384, 512))

FLOPS = 2 * 2 * 512 * 512 * 512


def entries(lst, a, b):
    return lst[:, a // 16 : b // 16]


def tile_picked_laypolarhop_none_po_kernel(
    tc, x_words, x_scales, w1_words, w1_scales, gn, w2_words, w2_scales, offs, n1, n2, n3, n4, out_0, out_1, out_2
):
    nc = tc.nc
    with ExitStack() as ctx:
        sb = ctx.enter_context(tc.tile_pool(name="sb", bufs=1))
        relay = ctx.enter_context(tc.tile_pool(name="relay", bufs=1))
        table = ctx.enter_context(tc.tile_pool(name="table", bufs=1))
        psum = ctx.enter_context(tc.psum_pool(name="psum", bufs=8))

        offs_t = sb.tile([P, S // 16], U16, name="offs_t")
        n1_t = sb.tile([P, W // 16], U16, name="n1_t")
        n2_t = sb.tile([P, W // 16], U16, name="n2_t")
        n3_t = sb.tile([P, S // 16], U16, name="n3_t")
        n4_t = sb.tile([P, S // 16], U16, name="n4_t")

        xw = table.tile([P, T], U32, name="xw", align_bytes=64, offset=S)
        xs = sb.tile([P, T], U8, name="xs", align_bytes=64)
        w1_raw = sb.tile([P, 2 * S], U8, name="w1_raw", align_bytes=64)
        w2_raw = sb.tile([P, 2 * S], U8, name="w2_raw", tag="pair0", align_bytes=64)
        s1_raw = table.tile([P, S], U8, name="s1_raw", align_bytes=64, offset=0)
        s2_raw = sb.tile([P, S], U8, name="s2_raw", align_bytes=64)
        gain = sb.tile([P, PACK], F32, name="gain")

        def load_scales(engine, tile, rows, quadrants):
            for q in quadrants:
                src = rows[0, 4 * q : 4 * q + 4, :].bitcast(I32)
                engine.dma_start(out=tile[32 * q : 32 * q + 32, :].bitcast(I32), in_=src.unsqueeze(0).to_broadcast([8, 4, src.shape[1]]))

        nc.sync.dma_start(out=w1_raw[:].bitcast(I32), in_=w1_words[0].bitcast(I32))
        nc.sync.dma_start(out=offs_t[:], in_=offs)
        load_scales(nc.sync, xs, x_scales, range(4))
        load_scales(nc.sync, s1_raw, w1_scales, range(1))
        nc.sync.dma_start(out=xw[:].bitcast(I32), in_=x_words[0].rearrange("p c r -> p (c r)").bitcast(I32))
        load_scales(nc.sync, s1_raw, w1_scales, range(1, 4))
        nc.sync.dma_start(out=w2_raw[:].bitcast(I32), in_=w2_words[0].bitcast(I32))
        nc.sync.dma_start(out=n1_t[:], in_=n1)
        nc.sync.dma_start(out=n2_t[:], in_=n2)
        nc.sync.dma_start(out=gain[:], in_=gn.rearrange("(p t) o -> p (t o)", t=PACK))
        load_scales(nc.sync, s2_raw, w2_scales, range(4))
        nc.sync.dma_start(out=n3_t[:], in_=n3)
        nc.sync.dma_start(out=n4_t[:], in_=n4)

        ident = sb.tile([P, P], F32, name="ident")
        make_identity(nc, ident[:])

        def deal_words(raw, dealt):
            nc.vector.tensor_copy(out=dealt[:], in_=raw[:].rearrange("p (m t b) -> p t m b", t=PACK, b=2))
            return [dealt[:, t].rearrange("p m b -> p (m b)") for t in range(PACK)]

        def deal_scales(raw, dealt):
            nc.vector.tensor_copy(out=dealt[:], in_=raw[:].rearrange("p (m t) -> p t m", t=PACK))
            return [dealt[:, t] for t in range(PACK)]

        def product(acc, words, scales, codes, code_scales):
            nc.tensor.matmul_mx(out=acc, lhsT=words.bitcast(FP4X4), lhsT_scale=scales, rhs=codes.bitcast(FP8X4), rhs_scale=code_scales, start=True, stop=True)

        w1 = deal_words(w1_raw, sb.tile([P, PACK, P, 2], U8, name="w1_dealt", align_bytes=64))
        gs = sb.tile([P, S], U8, name="gs", align_bytes=64)
        nc.vector.tensor_copy(out=gs[:], in_=xs[:].indirect(offs_t[:]))
        gw = sb.tile([P, S], U32, name="gw", align_bytes=64)
        y = [sb.tile([P, S], F32, name="y%d" % t, tag="y%d" % t, align_bytes=64) for t in range(PACK - 1)]
        y.append(relay.tile([P, S], F32, name="y3", offset=1024))
        for a in (0, HALF):
            cols = slice(a, a + HALF)
            nc.vector.tensor_copy(out=gw[:, cols], in_=xw[:].indirect(entries(offs_t, a, a + HALF)))
            if a == 0:
                s1 = deal_scales(s1_raw, sb.tile([P, PACK, P], U8, name="s1_dealt", align_bytes=64))
            acc = psum.tile([P, S], F32, name="acc")
            product(acc[:, :HALF], w1[0], s1[0], gw[:, cols], gs[:, cols])
            nc.scalar.copy(out=y[0][:, cols], in_=acc[:, :HALF])
        w2 = deal_words(w2_raw, table.tile([P, PACK, P, 2], U8, name="w2_dealt", align_bytes=64, offset=0))
        for t in range(1, PACK):
            acc = psum.tile([P, S], F32, name="acc")
            product(acc[:], w1[t], s1[t], gw[:], gs[:])
            nc.scalar.copy(out=y[t][:], in_=acc[:])


        pair = [sb.tile([P, 2 * W], F32, name="pair%d" % t, tag="pair%d" % t, align_bytes=64) for t in range(PACK)]
        win = [sb.tile([P, 2 * S], F32, name="win%d" % t) for t in range(PACK)]
        squares = [win[t][:, S:] for t in range(PACK)]
        turned = [sb.tile([P, W], F32, name="turned%d" % t, tag="turned%d" % t, align_bytes=64) for t in range(PACK)]
        dt = [relay.tile([P, S], F32, name="dt%d" % t, offset=2048 * t) for t in range(2)]
        dt.extend(sb.tile([P, S], F32, name="dt%d" % t, tag="dt%d" % t, align_bytes=64) for t in range(2, PACK))

        def fetch(t):
            nc.vector.tensor_scalar(out=pair[t][:, :W], in0=y[t][:].indirect(n1_t[:]), scalar1=-0.5, scalar2=0.0, op0=ALU.mult, op1=ALU.add)
            nc.vector.tensor_copy(out=pair[t][:, W:], in_=y[t][:].indirect(n2_t[:]))
            nc.scalar.activation(out=squares[t][:, :W], in_=pair[t][:, :W], func=ACT.Square, scale=2.0)
            nc.scalar.activation(out=squares[t][:, W:], in_=pair[t][:, W:], func=ACT.Square)

        def put_rb(t):
            nc.vector.tensor_tensor(out=dt[t][:].indirect(n2_t[:]), in0=pair[t][:, W:], in1=pair[t][:, :W], op=ALU.add)

        def root(t):
            total = psum.tile([P, S], F32, name="acc")
            for a in (0, P):
                for u in range(2):
                    nc.tensor.matmul(out=total[:, a : a + P], lhsT=squares[t][:, u * W + a : u * W + a + P], rhs=ident[:], is_transpose=True, start=(u == 0), stop=(u == 1))
            nc.scalar.activation(out=turned[t][:], in_=total[:, :W], func=ACT.Sqrt, bias=0.25)
            back = psum.tile([P, S], F32, name="acc")
            for a in (0, P):
                nc.tensor.transpose(back[:, a : a + P], turned[t][:, a : a + P], ident[:])
            nc.scalar.copy(out=ra[:, t, :], in_=back[:, :W])

        ra = sb.tile([P, PACK, W], F32, name="ra")
        fetch(0)
        for t in range(PACK):
            if t + 1 < PACK:
                fetch(t + 1)
            root(t)
        for t in range(PACK):
            put_rb(t)
        s2 = deal_scales(s2_raw, sb.tile([P, PACK, P], U8, name="s2_dealt", tag="y2", align_bytes=64))
        z_all = sb.tile([P, 2, HALF, PACK], BF16, name="z_all", tag="turned3", align_bytes=64)
        z = [z_all[:, h] for h in range(2)]
        for t in range(PACK):
            nc.vector.tensor_copy(out=dt[t][:].indirect(n1_t[:]), in_=ra[:, t, :])
            for h in range(2):
                src = dt[t][:, h * HALF : (h + 1) * HALF]
                if h == 1 and t >= 2:
                    nc.vector.tensor_scalar(out=z[h][:, :, t], in0=src, scalar1=gain[:, t : t + 1], scalar2=None, op0=ALU.mult)
                else:
                    nc.scalar.activation(out=z[h][:, :, t], in_=src, func=ACT.Copy, scale=gain[:, t : t + 1])

        zq = [sb.tile([P, HALF], U32, name="zq%d" % h, align_bytes=64) for h in range(2)]
        zs = [sb.tile([P, HALF], U8, name="zs%d" % h, align_bytes=64) for h in range(2)]
        hh = [sb.tile([P, S], F32, name="hh%d" % t) for t in range(PACK)]
        for h in (1, 0):
            nc.vector.quantize_mx(out=zq[h][:].bitcast(FP8X4), scales=zs[h][:], in_=z[h].rearrange("p c t -> p (c t)"))
            cols = slice(h * HALF, (h + 1) * HALF)
            acc = psum.tile([P, S], F32, name="acc")
            product(acc[:, :HALF], w2[0], s2[0], zq[h][:], zs[h][:])
            nc.scalar.activation(out=win[0][:, cols], in_=acc[:, :HALF], func=ACT.Copy, scale=-0.5)
            (nc.vector.tensor_copy if h else nc.scalar.copy)(out=hh[0][:, cols], in_=acc[:, :HALF])


        def second_layer(t):
            acc = psum.tile([P, S], F32, name="acc")
            for h in (1, 0):
                product(acc[:, h * HALF : (h + 1) * HALF], w2[t], s2[t], zq[h][:], zs[h][:])
            nc.scalar.activation(out=win[t][:, :S], in_=acc[:], func=ACT.Copy, scale=-0.5)
            nc.scalar.copy(out=hh[t][:], in_=acc[:])

        neg_st = [sb.tile([P, S], F32, name="neg_st%d" % t) for t in range(PACK)]
        copies = [sb.tile([P, PACK, HALF], F32, name="copies%d" % h, tag="copies%d" % h, align_bytes=64) for h in range(2)]

        def first_hop(t):
            for a, b in ((HALF, S), (0, HALF)) if t == 0 else ((0, S),):
                nc.vector.tensor_tensor(out=neg_st[t][:, a:b], in0=win[t][:].indirect(entries(n3_t, a, b)), in1=hh[t][:, a:b], op=ALU.subtract)

        res_first = sb.tile([P, PACK, HALF], F32, name="res_first")
        res = [res_first[:]]
        out_scales = sb.tile([P, S], U8, name="out_scales", align_bytes=64)
        out_rows = out_0.rearrange("(p t) j -> p t j", t=PACK)
        out_words = out_1[0].rearrange("p c r -> p (c r)").bitcast(I32)

        def copy_st(t, a, b):
            nc.scalar.copy(out=copies[a // HALF][:, t, :], in_=neg_st[t][:, a:b])

        def second_hop(c, t):
            a, b = OUT_CHUNKS[c]
            nc.vector.tensor_tensor(out=res[c][:, t, :], in0=neg_st[t][:].indirect(entries(n4_t, a, b)), in1=copies[a // HALF][:, t, a % HALF : a % HALF + b - a], op=ALU.subtract)

        def regroup(c, copy):
            a, b = OUT_CHUNKS[c]
            nc.sync.dma_start(out=out_rows[:, :, a:b], in_=res[c])
            grouped = sb.tile([P, b - a, PACK], BF16, name="grouped%d" % c, align_bytes=64)
            copy(out=grouped[:].rearrange("p (c i) t -> p c t i", i=4), in_=res[c].rearrange("p t (c i) -> p c t i", i=4))
            return grouped

        def quantise_out(c, grouped):
            a, b = OUT_CHUNKS[c]
            codes = sb.tile([P, b - a], U32, name="codes%d" % c, align_bytes=64)
            nc.vector.quantize_mx(out=codes[:].bitcast(FP8X4), scales=out_scales[:, a:b], in_=grouped[:].rearrange("p c t -> p (c t)"))
            nc.sync.dma_start(out=out_words[:, a:b], in_=codes[:].bitcast(I32))

        second_layer(1)
        first_hop(0)
        copy_st(0, 0, HALF)
        for t in range(1, PACK):
            if t + 1 < PACK:
                second_layer(t + 1)
            first_hop(t)
            copy_st(t, 0, HALF)
            second_hop(0, t - 1)
        second_hop(0, PACK - 1)
        for t in range(PACK):
            copy_st(t, HALF, S)
        res_rest = sb.tile([P, 2, PACK, P], F32, name="res_rest", tag="copies0", align_bytes=64)
        res.extend([res_rest[:, 0], res_rest[:, 1]])
        g0 = regroup(0, nc.scalar.copy)
        for t in range(PACK):
            second_hop(1, t)
        quantise_out(0, g0)
        g1 = regroup(1, nc.scalar.copy)
        for t in range(PACK):
            second_hop(2, t)
        quantise_out(1, g1)
        g2 = regroup(2, nc.vector.tensor_copy)
        quantise_out(2, g2)
        for q in range(4):
            engine = nc.scalar if q % 2 else nc.sync
            engine.dma_start(out=out_2[0, 4 * q : 4 * q + 4, :].bitcast(I32), in_=out_scales[32 * q : 32 * q + 4, :].bitcast(I32))
